import numpy as np
import ml_dtypes


def mxq(x, axis, fmt="e4m3"):
    dtype, down = {"e4m3": (ml_dtypes.float8_e4m3fn, 7), "e5m2": (ml_dtypes.float8_e5m2, 14)}[fmt]
    v = np.moveaxis(np.asarray(x, np.float32).astype(ml_dtypes.bfloat16).astype(np.float64), axis, -1)
    blocks = v.reshape(v.shape[:-1] + (-1, 32))
    amax = np.abs(blocks).max(-1, keepdims=True)
    byte = np.maximum(np.where(amax > 0, np.frexp(amax)[1] - 1 + 127, 0) - down, 1)
    scale = np.exp2(byte - 127.0)
    codes = (blocks / scale).astype(np.float32).astype(dtype).astype(np.float64)
    return np.moveaxis((codes * scale).reshape(v.shape), -1, axis)


WIDE = False


def mx_kscale(k):
    if not WIDE:
        return np.ones(k)
    levels = np.array([10, -10, 5, -5, 0])
    if k % 512:
        return np.exp2(np.random.permutation(np.resize(levels, k // 32))).repeat(32)
    a = np.empty((k // 512, 16))
    for p in range(k // 512):
        a[p, :8] = np.random.permutation(np.resize(levels, 8))
        for g in range(8):
            far = levels[np.abs(levels - a[p, g]) >= 10]
            a[p, g + 8] = far[np.random.randint(len(far))]
    return np.exp2(a.ravel()).repeat(32)


def f64(x):
    return np.asarray(x).astype(np.float64)


def striped(idx):
    return np.tile(idx.reshape(-1, 16).T, (8, 1)).astype(np.uint16)


def unstriped(offs):
    return offs[:16].T.reshape(-1).astype(np.int64)


E2M1 = np.array([0.0, 0.5, 1.0, 1.5, 2.0, 3.0, 4.0, 6.0, -0.0, -0.5, -1.0, -1.5, -2.0, -3.0, -4.0, -6.0])


def pack_weight(w, fmt):
    k, n = w.shape
    w = f64(np.asarray(w, np.float32).astype(ml_dtypes.bfloat16)).reshape(k // 32, 32, n)
    amax = np.abs(w).max(1)
    if fmt == "e4m3":
        byte = np.frexp(amax)[1] - 1 + 127 - 7
    else:
        mant, ex = np.frexp(amax / 6.0)
        byte = np.where(mant > 0.5, ex, ex - 1) + 127
    byte = np.clip(np.where(amax > 0, byte, 1), 1, 254)
    scaled = (w * np.exp2(127.0 - byte)[:, None, :]).reshape(k, n).astype(np.float32)
    by_word = np.ascontiguousarray(scaled.reshape(k // 512, 128, 4, n).transpose(0, 1, 3, 2))
    if fmt == "e4m3":
        words = by_word.astype(ml_dtypes.float8_e4m3fn).view(np.uint8)
    else:
        c = by_word.astype(ml_dtypes.float4_e2m1fn).view(np.uint8) & 0xF
        words = (c[..., 0::2] | (c[..., 1::2] << 4)).reshape(k // 512, 128, 2 * n)
    return np.ascontiguousarray(words), np.ascontiguousarray(byte.astype(np.uint8).reshape(k // 512, 16, n))


def unpack_weight(words, scales, fmt):
    g, _, n = scales.shape
    words = np.ascontiguousarray(words).reshape(g, 128, n, -1)
    if fmt == "e4m3":
        vals = words.view(ml_dtypes.float8_e4m3fn).astype(np.float64)
    else:
        nib = np.empty((g, 128, n, 4), np.uint8)
        nib[..., 0::2] = words & 0xF
        nib[..., 1::2] = words >> 4
        vals = E2M1[nib]
    vals = vals * np.repeat(np.exp2(scales.astype(np.float64) - 127.0), 8, axis=1)[..., None]
    return vals.transpose(0, 1, 3, 2).reshape(g * 512, n)


def gelu(v):
    return 0.5 * v * (1.0 + np.tanh(np.sqrt(2.0 / np.pi) * (v + 0.044715 * v**3)))


K, H, T, S, P = 512, 1536, 4096, 1024, 512


def setup_inputs():
    n = np.random.standard_normal
    s = mx_kscale(K)[:, None]
    u = mx_kscale(H)[:, None]
    tab_words, tab_scales = pack_weight(n((K, T)) * s, "e4m3")
    w2_words, w2_scales = pack_weight(0.8 * n((K, H)) / np.sqrt(K) / s, "e2m1")
    return {
        "tab_words": tab_words,
        "tab_scales": tab_scales,
        "offs": striped(np.random.permutation(T)[:S]),
        "pos1": striped(np.random.permutation(S)[:P]),
        "pos2": striped(np.random.permutation(S)[:P]),
        "w1": (1.5 * n((K, H)) / np.sqrt(K) / s).astype(np.float32),
        "w2_words": w2_words,
        "w2_scales": w2_scales,
        "gain": (np.random.uniform(0.6, 1.4, H) * u[:, 0]).astype(np.float32),
        "dh": (n(H) / np.sqrt(H) / u[:, 0] ** 2).astype(np.float32),
        "wr": (n((H, P)) * u).astype(np.float32),
    }


def reference(tab_words, tab_scales, offs, pos1, pos2, w1, w2_words, w2_scales, gain, dh, wr):
    v = unpack_weight(tab_words, tab_scales, "e4m3")[:, unstriped(offs)]
    w2 = unpack_weight(w2_words, w2_scales, "e2m1")
    bounded = np.tanh(mxq(f64(w1), 0, "e4m3").T @ v)
    linear = w2.T @ v
    h = (bounded + linear) * f64(gain)[:, None]
    x1 = mxq(h[:, unstriped(pos1)], 0, "e4m3")
    x2 = mxq(np.abs(h[:, unstriped(pos2)]) * f64(dh)[:, None], 0, "e4m3")
    e = x1.T @ x2
    ref = mxq(f64(wr), 0, "e4m3").T @ x2
    return np.maximum(e, ref)

@@ -1,0 +1,245 @@
+from contextlib import ExitStack
+
+import concourse.mybir as mybir
+
+K, H, T, S, NP = 512, 1536, 4096, 1024, 512
+FLOPS = 2 * 2 * K * H * S + 2 * 2 * H * NP * NP
+
+F32 = mybir.dt.float32
+BF16 = mybir.dt.bfloat16
+I32 = mybir.dt.int32
+U32 = mybir.dt.uint32
+U16 = mybir.dt.uint16
+U8 = mybir.dt.uint8
+FP8X4 = mybir.dt.float8_e4m3fn_x4
+FP4X4 = mybir.dt.float4_e2m1fn_x4
+ACT = mybir.ActivationFunctionType
+ALU = mybir.AluOpType
+
+P = 128
+PACK = 4
+PASS = P * PACK
+NB = H // PASS
+BANK = 512
+HALVES = S // BANK
+MT = NP // P
+
+
+def tile_list_pair_seat_harmony_kernel(
+    tc, tab_words, tab_scales, offs, pos1, pos2, w1, w2_words, w2_scales, gain, dh, wr, out
+):
+    nc = tc.nc
+    with ExitStack() as ctx:
+        keep = ctx.enter_context(tc.tile_pool(name="keep", bufs=1))
+        ring = ctx.enter_context(tc.tile_pool(name="ring", bufs=2))
+        picks = ctx.enter_context(tc.tile_pool(name="picks", bufs=3))
+        wins = ctx.enter_context(tc.tile_pool(name="wins", bufs=5))
+        psum = ctx.enter_context(tc.psum_pool(name="psum", bufs=1))
+
+        offs_t = keep.tile([P, S // 16], U16, name="offs_t")
+        pos1_t = keep.tile([P, NP // 16], U16, name="pos1_t")
+        pos2_t = keep.tile([P, NP // 16], U16, name="pos2_t")
+        tabw = keep.tile([P, T], U32, name="tabw", align_bytes=64)
+        tabs = keep.tile([P, T], U8, name="tabs", align_bytes=64)
+        w2w = keep.tile([P, 2 * H], U8, name="w2w", align_bytes=64)
+        w2s = keep.tile([P, H], U8, name="w2s", align_bytes=64)
+        gain_t = keep.tile([P, NB, PACK], F32, name="gain_t")
+        dh_t = keep.tile([P, NB, PACK], F32, name="dh_t")
+        w1_raw = [keep.tile([P, PACK, PASS], F32, name="w1_raw%d" % b) for b in range(NB)]
+        wr_raw = [keep.tile([P, PACK, NP], F32, name="wr_raw%d" % b) for b in range(NB)]
+
+        nc.vector.memset(w2s[:].bitcast(I32), 0)
+        nc.vector.memset(tabs[:].bitcast(I32), 0)
+
+        def load_scales(tile, rows):
+            for q in range(4):
+                nc.sync.dma_start(tile[32 * q : 32 * q + 4, :].bitcast(I32), rows[4 * q : 4 * q + 4, :].bitcast(I32))
+
+        w1_rows = w1.rearrange("(p j) c -> p j c", j=PACK)
+        wr_rows = wr.rearrange("(b p j) m -> b p j m", p=P, j=PACK)
+        nc.sync.dma_start(offs_t[:], offs)
+        nc.sync.dma_start(w2w[:].bitcast(I32), w2_words[0].bitcast(I32))
+        load_scales(w2s, w2_scales[0])
+        nc.sync.dma_start(tabw[:].bitcast(I32), tab_words[0].rearrange("p t i -> p (t i)").bitcast(I32))
+        load_scales(tabs, tab_scales[0])
+        nc.sync.dma_start(w1_raw[0][:], w1_rows[:, :, 0:PASS])
+        nc.sync.dma_start(gain_t[:], gain.rearrange("(b p t) -> p b t", p=P, t=PACK))
+        nc.sync.dma_start(dh_t[:], dh.rearrange("(b p t) -> p b t", p=P, t=PACK))
+        nc.sync.dma_start(pos1_t[:], pos1)
+        nc.sync.dma_start(pos2_t[:], pos2)
+        for b in range(1, NB):
+            nc.sync.dma_start(w1_raw[b][:], w1_rows[:, :, b * PASS : (b + 1) * PASS])
+        for b in range(NB):
+            nc.sync.dma_start(wr_raw[b][:], wr_rows[b])
+
+        w2_codes = keep.tile([P, 2 * H], U8, name="w2_codes", align_bytes=64)
+        w2_sc = keep.tile([P, H], U8, name="w2_sc", align_bytes=64)
+        nc.vector.tensor_copy(
+            w2_codes[:].rearrange("p (b t q e) -> p b t q e", b=NB, t=PACK, e=2),
+            w2w[:].rearrange("p (b q t e) -> p b t q e", b=NB, t=PACK, e=2),
+        )
+        nc.vector.tensor_copy(
+            w2_sc[:].rearrange("p (b t q) -> p t b q", b=NB, t=PACK),
+            w2s[:].rearrange("p (b q t) -> p t b q", b=NB, t=PACK),
+        )
+
+        v_codes = [keep.tile([P, BANK], U32, name="v_codes%d" % h, align_bytes=64) for h in range(HALVES)]
+        v_sc = [keep.tile([P, BANK], U8, name="v_sc%d" % h, align_bytes=64) for h in range(HALVES)]
+        per = BANK // 16
+        for h in range(HALVES):
+            part = offs_t[:, h * per : (h + 1) * per]
+            nc.vector.tensor_copy(v_codes[h][:], tabw[:].indirect(part))
+            nc.vector.tensor_copy(v_sc[h][:], tabs[:].indirect(part))
+
+        def planes(name, width):
+            codes = [keep.tile([P, width], U32, name="%s_codes%d" % (name, b), align_bytes=64) for b in range(NB)]
+            sc = [keep.tile([P, width], U8, name="%s_sc%d" % (name, b), align_bytes=64) for b in range(NB)]
+            return codes, sc
+
+        w1_codes, w1_sc = planes("w1", PASS)
+        wr_codes, wr_sc = planes("wr", NP)
+        x1_codes, x1_sc = planes("x1", NP)
+        x2_codes, x2_sc = planes("x2", NP)
+        w1_il, wr_il, x1_il, x2_il, x1_rows, x2_rows = {}, {}, {}, {}, {}, {}
+
+        def new_il(name):
+            return ring.tile([P, PACK * NP], BF16, name=name, align_bytes=64)
+
+        def new_rows(name):
+            return ring.tile([P, PACK, NP], BF16, name=name)
+
+        def quantize(codes, sc, il, c0, c1):
+            nc.vector.quantize_mx(out=codes[:, c0:c1].bitcast(FP8X4), scales=sc[:, c0:c1], in_=il[:, PACK * c0 : PACK * c1])
+
+        def cast_w1(b):
+            w1_il[b] = new_il("w1_il")
+            nc.scalar.copy(
+                w1_il[b][:].rearrange("p (t q j) -> p q j t", t=PACK, j=PACK),
+                w1_raw[b][:].rearrange("p j (q t) -> p q j t", t=PACK),
+            )
+
+        def il_views(il, rows, c0, c1):
+            dst = il[:, PACK * c0 : PACK * c1].rearrange("p (c i t) -> p c t i", i=4, t=PACK)
+            srcv = rows[:, :, c0:c1].rearrange("p t (c i) -> p c t i", i=4)
+            return dst, srcv
+
+        def cast_wr(b):
+            wr_il[b] = new_il("wr_il")
+            dst, srcv = il_views(wr_il[b], wr_raw[b], 0, NP)
+            nc.gpsimd.tensor_scalar(dst, srcv, 1.0, 0.0, ALU.mult, ALU.add)
+
+        def interleave(il, rows, c0, c1):
+            dst, srcv = il_views(il, rows, c0, c1)
+            nc.scalar.copy(dst, srcv)
+
+        windows = {}
+
+        def first_stage(s):
+            b, t = divmod(s, PACK)
+            cols = slice(t * P, (t + 1) * P)
+            c0 = b * PASS + t * P
+            win = wins.tile([P, S], F32, name="win")
+            windows[s] = win
+            for h in range(HALVES):
+                bank = (s % 2) * 4 + 2 * h
+                pa = psum.tile([P, BANK], F32, name="bank%d" % bank)
+                pl = psum.tile([P, BANK], F32, name="bank%d" % (bank + 1))
+                nc.tensor.matmul_mx(
+                    out=pa[:], lhsT=w1_codes[b][:, cols].bitcast(FP8X4), lhsT_scale=w1_sc[b][:, cols],
+                    rhs=v_codes[h][:].bitcast(FP8X4), rhs_scale=v_sc[h][:], start=True, stop=True,
+                )
+                nc.tensor.matmul_mx(
+                    out=pl[:], lhsT=w2_codes[:, 2 * c0 : 2 * (c0 + P)].bitcast(FP4X4), lhsT_scale=w2_sc[:, c0 : c0 + P],
+                    rhs=v_codes[h][:].bitcast(FP8X4), rhs_scale=v_sc[h][:], start=True, stop=True,
+                )
+                bounded = picks.tile([P, BANK], F32, name="bounded")
+                nc.scalar.activation(bounded[:], pa[:], ACT.Tanh)
+                nc.vector.tensor_tensor(win[:, h * BANK : (h + 1) * BANK], pl[:], bounded[:], ALU.add)
+
+        def pick_x1(s):
+            b, t = divmod(s, PACK)
+            if t == 0:
+                x1_rows[b] = new_rows("x1_rows")
+            g1 = picks.tile([P, NP], F32, name="g1")
+            nc.vector.tensor_copy(g1[:], windows[s][:].indirect(pos1_t[:]))
+            nc.gpsimd.tensor_scalar(x1_rows[b][:, t, :], g1[:], gain_t[:, b, t : t + 1], 0.0, ALU.mult, ALU.add)
+
+        def pick_x2(s):
+            b, t = divmod(s, PACK)
+            if t == 0:
+                x2_rows[b] = new_rows("x2_rows")
+            g2 = picks.tile([P, NP], F32, name="g2")
+            nc.vector.tensor_copy(g2[:], windows[s][:].indirect(pos2_t[:]))
+            size = picks.tile([P, NP], F32, name="size")
+            nc.scalar.activation(size[:], g2[:], ACT.Abs, scale=gain_t[:, b, t : t + 1])
+            nc.gpsimd.tensor_scalar(x2_rows[b][:, t, :], size[:], dh_t[:, b, t : t + 1], 0.0, ALU.mult, ALU.add)
+
+        cast_w1(0)
+        quantize(w1_codes[0], w1_sc[0], w1_il[0], 0, PASS)
+        slices = NB * PACK
+        last = NB - 1
+        for s in range(slices + 1):
+            b, t = divmod(s, PACK)
+            if s < slices:
+                first_stage(s)
+            if s >= 1:
+                pick_x2(s - 1)
+                if s - 1 < last * PACK:
+                    pick_x1(s - 1)
+            if s < slices:
+                if t == 0:
+                    if b + 1 < NB:
+                        cast_w1(b + 1)
+                    cast_wr(b)
+                if t == 1 and b >= 1:
+                    x2_il[b - 1] = new_il("x2_il")
+                    interleave(x2_il[b - 1], x2_rows[b - 1], 0, NP)
+                if t == 2:
+                    if b + 1 < NB:
+                        quantize(w1_codes[b + 1], w1_sc[b + 1], w1_il[b + 1], 0, PASS)
+                    quantize(wr_codes[b], wr_sc[b], wr_il[b], 0, NP)
+                    if b >= 1:
+                        x1_il[b - 1] = new_il("x1_il")
+                        interleave(x1_il[b - 1], x1_rows[b - 1], 0, NP)
+                if t == 3 and b >= 1:
+                    quantize(x2_codes[b - 1], x2_sc[b - 1], x2_il[b - 1], 0, NP)
+                    quantize(x1_codes[b - 1], x1_sc[b - 1], x1_il[b - 1], 0, NP)
+
+        ref_ps = [psum.tile([P, BANK], F32, name="bank%d" % m) for m in range(MT)]
+        e_ps = [psum.tile([P, BANK], F32, name="bank%d" % (MT + m)) for m in range(MT)]
+
+        def second_pass(acc, codes, sc, b, m):
+            cols = slice(m * P, (m + 1) * P)
+            nc.tensor.matmul_mx(
+                out=acc[m][:], lhsT=codes[b][:, cols].bitcast(FP8X4), lhsT_scale=sc[b][:, cols],
+                rhs=x2_codes[b][:].bitcast(FP8X4), rhs_scale=x2_sc[b][:], start=(b == 0), stop=(b == last),
+            )
+
+        for b in range(last):
+            for m in range(MT):
+                second_pass(ref_ps, wr_codes, wr_sc, b, m)
+        for b in range(last):
+            for m in range(MT):
+                second_pass(e_ps, x1_codes, x1_sc, b, m)
+
+        x2_il[last] = new_il("x2_il")
+        x1_il[last] = new_il("x1_il")
+        interleave(x2_il[last], x2_rows[last], 0, NP)
+        for t in range(PACK):
+            pick_x1(last * PACK + t)
+            if t == 2:
+                quantize(x2_codes[last], x2_sc[last], x2_il[last], 0, NP)
+        ref_sb = [keep.tile([P, BANK], F32, name="ref_sb%d" % m) for m in range(MT)]
+        for m in range(MT):
+            second_pass(ref_ps, wr_codes, wr_sc, last, m)
+        for m in range(MT):
+            interleave(x1_il[last], x1_rows[last], m * P, (m + 1) * P)
+            nc.scalar.copy(ref_sb[m][:], ref_ps[m][:])
+        for m in range(MT + 1):
+            if m < MT:
+                quantize(x1_codes[last], x1_sc[last], x1_il[last], m * P, (m + 1) * P)
+                second_pass(e_ps, x1_codes, x1_sc, last, m)
+            if m >= 1:
+                res = keep.tile([P, BANK], F32, name="res%d" % (m - 1))
+                nc.vector.tensor_tensor(res[:], e_ps[m - 1][:], ref_sb[m - 1][:], ALU.max)
+                nc.sync.dma_start(out[(m - 1) * P : m * P, :], res[:])

@@ -23,6 +23,19 @@ NB = H // PASS
 BANK = 512
 HALVES = S // BANK
 MT = NP // P
+AHEAD = 3
+TXT = 3
+RING = 4
+WINDOWS = 6
+X2S = 11
+WR_AT = [4, 7, 8]
+LAG = 0
+X1S = 8
+ILV = 4
+CUT = 4
+CUTX = 2
+W1_AT = 1
+TIE = 1
 
 
 def tile_list_pair_seat_harmony_kernel(
@@ -32,8 +45,6 @@ def tile_list_pair_seat_harmony_kernel(
     with ExitStack() as ctx:
         keep = ctx.enter_context(tc.tile_pool(name="keep", bufs=1))
         ring = ctx.enter_context(tc.tile_pool(name="ring", bufs=2))
-        picks = ctx.enter_context(tc.tile_pool(name="picks", bufs=3))
-        wins = ctx.enter_context(tc.tile_pool(name="wins", bufs=5))
         psum = ctx.enter_context(tc.psum_pool(name="psum", bufs=1))
 
         offs_t = keep.tile([P, S // 16], U16, name="offs_t")
@@ -41,55 +52,58 @@ def tile_list_pair_seat_harmony_kernel(
         pos2_t = keep.tile([P, NP // 16], U16, name="pos2_t")
         tabw = keep.tile([P, T], U32, name="tabw", align_bytes=64)
         tabs = keep.tile([P, T], U8, name="tabs", align_bytes=64)
-        w2w = keep.tile([P, 2 * H], U8, name="w2w", align_bytes=64)
         w2s = keep.tile([P, H], U8, name="w2s", align_bytes=64)
         gain_t = keep.tile([P, NB, PACK], F32, name="gain_t")
         dh_t = keep.tile([P, NB, PACK], F32, name="dh_t")
-        w1_raw = [keep.tile([P, PACK, PASS], F32, name="w1_raw%d" % b) for b in range(NB)]
-        wr_raw = [keep.tile([P, PACK, NP], F32, name="wr_raw%d" % b) for b in range(NB)]
+        w2_codes = keep.tile([P, 2 * H], U8, name="w2_codes", align_bytes=64)
+        w2_sc = keep.tile([P, H], U8, name="w2_sc", align_bytes=64)
 
-        nc.vector.memset(w2s[:].bitcast(I32), 0)
-        nc.vector.memset(tabs[:].bitcast(I32), 0)
+        def slot(name, shape, dtype):
+            return keep.tile(shape, dtype, name="slot_" + name, align_bytes=64)
 
-        def load_scales(tile, rows):
+        def load_scales(queue, tile, rows):
             for q in range(4):
-                nc.sync.dma_start(tile[32 * q : 32 * q + 4, :].bitcast(I32), rows[4 * q : 4 * q + 4, :].bitcast(I32))
+                queue.dma_start(tile[32 * q : 32 * q + 4, :].bitcast(I32), rows[4 * q : 4 * q + 4, :].bitcast(I32))
 
         w1_rows = w1.rearrange("(p j) c -> p j c", j=PACK)
         wr_rows = wr.rearrange("(b p j) m -> b p j m", p=P, j=PACK)
-        nc.sync.dma_start(offs_t[:], offs)
-        nc.sync.dma_start(w2w[:].bitcast(I32), w2_words[0].bitcast(I32))
-        load_scales(w2s, w2_scales[0])
-        nc.sync.dma_start(tabw[:].bitcast(I32), tab_words[0].rearrange("p t i -> p (t i)").bitcast(I32))
-        load_scales(tabs, tab_scales[0])
-        nc.sync.dma_start(w1_raw[0][:], w1_rows[:, :, 0:PASS])
-        nc.sync.dma_start(gain_t[:], gain.rearrange("(b p t) -> p b t", p=P, t=PACK))
-        nc.sync.dma_start(dh_t[:], dh.rearrange("(b p t) -> p b t", p=P, t=PACK))
-        nc.sync.dma_start(pos1_t[:], pos1)
-        nc.sync.dma_start(pos2_t[:], pos2)
-        for b in range(1, NB):
-            nc.sync.dma_start(w1_raw[b][:], w1_rows[:, :, b * PASS : (b + 1) * PASS])
-        for b in range(NB):
-            nc.sync.dma_start(wr_raw[b][:], wr_rows[b])
+        HALF = PASS // 2
 
-        w2_codes = keep.tile([P, 2 * H], U8, name="w2_codes", align_bytes=64)
-        w2_sc = keep.tile([P, H], U8, name="w2_sc", align_bytes=64)
-        nc.vector.tensor_copy(
-            w2_codes[:].rearrange("p (b t q e) -> p b t q e", b=NB, t=PACK, e=2),
-            w2w[:].rearrange("p (b q t e) -> p b t q e", b=NB, t=PACK, e=2),
-        )
-        nc.vector.tensor_copy(
-            w2_sc[:].rearrange("p (b t q) -> p t b q", b=NB, t=PACK),
-            w2s[:].rearrange("p (b q t) -> p t b q", b=NB, t=PACK),
-        )
+        nc.gpsimd.memset(w2s[:].bitcast(I32), 0)
+        nc.vector.memset(tabs[:].bitcast(I32), 0)
+        load_scales(nc.gpsimd, w2s, w2_scales[0])
+        nc.sync.dma_start(offs_t[:], offs)
+        nc.sync.dma_start(pos2_t[:], pos2)
+        nc.sync.dma_start(pos1_t[:], pos1)
+        w2w_first = slot("a", [P, 2 * PASS], U8)
+        nc.sync.dma_start(w2w_first[:].bitcast(I32), w2_words[0][:, 0 : 2 * PASS].bitcast(I32))
+        nc.sync.dma_start(tabw[:].bitcast(I32), tab_words[0].rearrange("p t i -> p (t i)").bitcast(I32))
+        w1_halves = [slot("b", [P, PACK, HALF], F32), slot("c", [P, PACK, HALF], F32)]
+        for u in range(2):
+            nc.sync.dma_start(w1_halves[u][:], w1_rows[:, :, u * HALF : (u + 1) * HALF])
+        load_scales(nc.scalar, tabs, tab_scales[0])
+
+        def deal_w2(b, words):
+            nc.gpsimd.tensor_copy(
+                w2_codes[:, 2 * b * PASS : 2 * (b + 1) * PASS].rearrange("p (t q e) -> p t q e", t=PACK, e=2),
+                words.rearrange("p (q t e) -> p t q e", t=PACK, e=2),
+            )
+            nc.gpsimd.tensor_copy(
+                w2_sc[:, b * PASS : (b + 1) * PASS].rearrange("p (t q) -> p t q", t=PACK),
+                w2s[:, b * PASS : (b + 1) * PASS].rearrange("p (q t) -> p t q", t=PACK),
+            )
+
+        deal_w2(0, w2w_first[:])
+        nc.gpsimd.dma_start(gain_t[:], gain.rearrange("(b p t) -> p b t", p=P, t=PACK))
+        nc.gpsimd.dma_start(dh_t[:], dh.rearrange("(b p t) -> p b t", p=P, t=PACK))
 
         v_codes = [keep.tile([P, BANK], U32, name="v_codes%d" % h, align_bytes=64) for h in range(HALVES)]
-        v_sc = [keep.tile([P, BANK], U8, name="v_sc%d" % h, align_bytes=64) for h in range(HALVES)]
         per = BANK // 16
+        parts = [offs_t[:, h * per : (h + 1) * per] for h in range(HALVES)]
         for h in range(HALVES):
-            part = offs_t[:, h * per : (h + 1) * per]
-            nc.vector.tensor_copy(v_codes[h][:], tabw[:].indirect(part))
-            nc.vector.tensor_copy(v_sc[h][:], tabs[:].indirect(part))
+            nc.vector.tensor_copy(v_codes[h][:], tabw[:].indirect(parts[h]))
+        v_sc = [keep.tile([P, BANK], U8, name="v_sc0", align_bytes=64)]
+        nc.vector.tensor_copy(v_sc[0][:], tabs[:].indirect(parts[0]))
 
         def planes(name, width):
             codes = [keep.tile([P, width], U32, name="%s_codes%d" % (name, b), align_bytes=64) for b in range(NB)]
@@ -111,11 +125,10 @@ def tile_list_pair_seat_harmony_kernel(
         def quantize(codes, sc, il, c0, c1):
             nc.vector.quantize_mx(out=codes[:, c0:c1].bitcast(FP8X4), scales=sc[:, c0:c1], in_=il[:, PACK * c0 : PACK * c1])
 
-        def cast_w1(b):
-            w1_il[b] = new_il("w1_il")
+        def cast_w1(b, raw, q0, q1):
             nc.scalar.copy(
-                w1_il[b][:].rearrange("p (t q j) -> p q j t", t=PACK, j=PACK),
-                w1_raw[b][:].rearrange("p j (q t) -> p q j t", t=PACK),
+                w1_il[b][:].rearrange("p (t q j) -> p q j t", t=PACK, j=PACK)[:, q0:q1],
+                raw.rearrange("p j (q t) -> p q j t", t=PACK),
             )
 
         def il_views(il, rows, c0, c1):
@@ -123,27 +136,26 @@ def tile_list_pair_seat_harmony_kernel(
             srcv = rows[:, :, c0:c1].rearrange("p t (c i) -> p c t i", i=4)
             return dst, srcv
 
-        def cast_wr(b):
-            wr_il[b] = new_il("wr_il")
-            dst, srcv = il_views(wr_il[b], wr_raw[b], 0, NP)
-            nc.gpsimd.tensor_scalar(dst, srcv, 1.0, 0.0, ALU.mult, ALU.add)
-
         def interleave(il, rows, c0, c1):
             dst, srcv = il_views(il, rows, c0, c1)
             nc.scalar.copy(dst, srcv)
 
         windows = {}
+        slices = NB * PACK
+        last = NB - 1
+
+        def half_row(s, h):
+            return keep.tile([P, BANK], F32, name="half%d_%d" % (s % RING, h))
 
         def first_stage(s):
             b, t = divmod(s, PACK)
             cols = slice(t * P, (t + 1) * P)
             c0 = b * PASS + t * P
-            win = wins.tile([P, S], F32, name="win")
+            win = keep.tile([P, S], F32, name="win%d" % (s % WINDOWS))
             windows[s] = win
             for h in range(HALVES):
-                bank = (s % 2) * 4 + 2 * h
-                pa = psum.tile([P, BANK], F32, name="bank%d" % bank)
-                pl = psum.tile([P, BANK], F32, name="bank%d" % (bank + 1))
+                pa = psum.tile([P, BANK], F32, name="bank%d" % h)
+                pl = psum.tile([P, BANK], F32, name="bank%d" % (HALVES * (1 + s % AHEAD) + h))
                 nc.tensor.matmul_mx(
                     out=pa[:], lhsT=w1_codes[b][:, cols].bitcast(FP8X4), lhsT_scale=w1_sc[b][:, cols],
                     rhs=v_codes[h][:].bitcast(FP8X4), rhs_scale=v_sc[h][:], start=True, stop=True,
@@ -152,7 +164,7 @@ def tile_list_pair_seat_harmony_kernel(
                     out=pl[:], lhsT=w2_codes[:, 2 * c0 : 2 * (c0 + P)].bitcast(FP4X4), lhsT_scale=w2_sc[:, c0 : c0 + P],
                     rhs=v_codes[h][:].bitcast(FP8X4), rhs_scale=v_sc[h][:], start=True, stop=True,
                 )
-                bounded = picks.tile([P, BANK], F32, name="bounded")
+                bounded = half_row(s, h)
                 nc.scalar.activation(bounded[:], pa[:], ACT.Tanh)
                 nc.vector.tensor_tensor(win[:, h * BANK : (h + 1) * BANK], pl[:], bounded[:], ALU.add)
 
@@ -160,7 +172,7 @@ def tile_list_pair_seat_harmony_kernel(
             b, t = divmod(s, PACK)
             if t == 0:
                 x1_rows[b] = new_rows("x1_rows")
-            g1 = picks.tile([P, NP], F32, name="g1")
+            g1 = keep.tile([P, NP], F32, name="size%d" % ((s - TIE) % (TIE + 2)))
             nc.vector.tensor_copy(g1[:], windows[s][:].indirect(pos1_t[:]))
             nc.gpsimd.tensor_scalar(x1_rows[b][:, t, :], g1[:], gain_t[:, b, t : t + 1], 0.0, ALU.mult, ALU.add)
 
@@ -168,42 +180,66 @@ def tile_list_pair_seat_harmony_kernel(
             b, t = divmod(s, PACK)
             if t == 0:
                 x2_rows[b] = new_rows("x2_rows")
-            g2 = picks.tile([P, NP], F32, name="g2")
+            g2 = half_row(s + 1, 0)
             nc.vector.tensor_copy(g2[:], windows[s][:].indirect(pos2_t[:]))
-            size = picks.tile([P, NP], F32, name="size")
+            size = keep.tile([P, NP], F32, name="size%d" % (s % (TIE + 2)))
             nc.scalar.activation(size[:], g2[:], ACT.Abs, scale=gain_t[:, b, t : t + 1])
-            nc.gpsimd.tensor_scalar(x2_rows[b][:, t, :], size[:], dh_t[:, b, t : t + 1], 0.0, ALU.mult, ALU.add)
+            if s >= X2S:
+                nc.scalar.activation(x2_rows[b][:, t, :], size[:], ACT.Copy, scale=dh_t[:, b, t : t + 1])
+            else:
+                nc.gpsimd.tensor_scalar(x2_rows[b][:, t, :], size[:], dh_t[:, b, t : t + 1], 0.0, ALU.mult, ALU.add)
 
-        cast_w1(0)
+        def prepare_w1(b):
+            raw = slot("a" if b == 1 else "c", [P, PACK, PASS], F32)
+            nc.sync.dma_start(raw[:], w1_rows[:, :, b * PASS : (b + 1) * PASS])
+            w1_il[b] = new_il("w1_il")
+            for u in range(CUT):
+                q0, q1 = u * P // CUT, (u + 1) * P // CUT
+                cast_w1(b, raw[:, :, PACK * q0 : PACK * q1], q0, q1)
+            quantize(w1_codes[b], w1_sc[b], w1_il[b], 0, PASS)
+
+        def prepare_wr(b):
+            raw = slot("aca"[b : b + 1], [P, PACK, NP], F32)
+            nc.sync.dma_start(raw[:], wr_rows[b])
+            wr_il[b] = new_il("wr_il")
+            for u in range(CUT):
+                interleave(wr_il[b], raw, u * NP // CUT, (u + 1) * NP // CUT)
+            quantize(wr_codes[b], wr_sc[b], wr_il[b], 0, NP)
+
+        def finish(il, name, rows, codes, sc, b):
+            il[b] = new_il(name)
+            for u in range(CUTX):
+                interleave(il[b], rows[b], u * NP // CUTX, (u + 1) * NP // CUTX)
+            quantize(codes[b], sc[b], il[b], 0, NP)
+
+        w1_il[0] = slot("d", [P, PACK * PASS], BF16)
+        for u in range(2):
+            cast_w1(0, w1_halves[u][:], u * P // 2, (u + 1) * P // 2)
         quantize(w1_codes[0], w1_sc[0], w1_il[0], 0, PASS)
-        slices = NB * PACK
-        last = NB - 1
-        for s in range(slices + 1):
-            b, t = divmod(s, PACK)
-            if s < slices:
-                first_stage(s)
-            if s >= 1:
-                pick_x2(s - 1)
-                if s - 1 < last * PACK:
-                    pick_x1(s - 1)
-            if s < slices:
-                if t == 0:
-                    if b + 1 < NB:
-                        cast_w1(b + 1)
-                    cast_wr(b)
-                if t == 1 and b >= 1:
-                    x2_il[b - 1] = new_il("x2_il")
-                    interleave(x2_il[b - 1], x2_rows[b - 1], 0, NP)
-                if t == 2:
-                    if b + 1 < NB:
-                        quantize(w1_codes[b + 1], w1_sc[b + 1], w1_il[b + 1], 0, PASS)
-                    quantize(wr_codes[b], wr_sc[b], wr_il[b], 0, NP)
-                    if b >= 1:
-                        x1_il[b - 1] = new_il("x1_il")
-                        interleave(x1_il[b - 1], x1_rows[b - 1], 0, NP)
-                if t == 3 and b >= 1:
-                    quantize(x2_codes[b - 1], x2_sc[b - 1], x2_il[b - 1], 0, NP)
-                    quantize(x1_codes[b - 1], x1_sc[b - 1], x1_il[b - 1], 0, NP)
+        v_sc.append(slot("d", [P, BANK], U8))
+        nc.vector.tensor_copy(v_sc[1][:], tabs[:].indirect(parts[1]))
+        w2w_rest = slot("b", [P, 2 * (H - PASS)], U8)
+        nc.sync.dma_start(w2w_rest[:].bitcast(I32), w2_words[0][:, 2 * PASS : 2 * H].bitcast(I32))
+        for b in range(1, NB):
+            deal_w2(b, w2w_rest[:, 2 * (b - 1) * PASS : 2 * b * PASS])
+
+        for i in range(slices + TXT):
+            if i < slices:
+                first_stage(i)
+                if i % PACK == W1_AT and i // PACK < last:
+                    prepare_w1(i // PACK + 1)
+                if i in WR_AT:
+                    prepare_wr(WR_AT.index(i))
+            s = i - TXT
+            if s >= 0:
+                b, t = divmod(s, PACK)
+                pick_x2(s)
+                if LAG <= s and s - LAG < last * PACK:
+                    pick_x1(s - LAG)
+                if t == PACK - 1:
+                    finish(x2_il, "x2_il", x2_rows, x2_codes, x2_sc, b)
+                    if b < last:
+                        finish(x1_il, "x1_il", x1_rows, x1_codes, x1_sc, b)
 
         ref_ps = [psum.tile([P, BANK], F32, name="bank%d" % m) for m in range(MT)]
         e_ps = [psum.tile([P, BANK], F32, name="bank%d" % (MT + m)) for m in range(MT)]
@@ -215,31 +251,53 @@ def tile_list_pair_seat_harmony_kernel(
                 rhs=x2_codes[b][:].bitcast(FP8X4), rhs_scale=x2_sc[b][:], start=(b == 0), stop=(b == last),
             )
 
-        for b in range(last):
-            for m in range(MT):
-                second_pass(ref_ps, wr_codes, wr_sc, b, m)
-        for b in range(last):
-            for m in range(MT):
-                second_pass(e_ps, x1_codes, x1_sc, b, m)
+        for acc, codes, sc in ((ref_ps, wr_codes, wr_sc), (e_ps, x1_codes, x1_sc)):
+            for b in range(last):
+                for m in range(MT):
+                    second_pass(acc, codes, sc, b, m)
 
-        x2_il[last] = new_il("x2_il")
+        x1_rows[last] = new_rows("x1_rows")
         x1_il[last] = new_il("x1_il")
-        interleave(x2_il[last], x2_rows[last], 0, NP)
-        for t in range(PACK):
-            pick_x1(last * PACK + t)
-            if t == 2:
-                quantize(x2_codes[last], x2_sc[last], x2_il[last], 0, NP)
-        ref_sb = [keep.tile([P, BANK], F32, name="ref_sb%d" % m) for m in range(MT)]
-        for m in range(MT):
+        ref_sb = [keep.tile([P, BANK], F32, name="ref%d" % m) for m in range(MT)]
+
+        late = [(slices - 1, 1), (slices - 1, 0), (slices, 0), (slices - 1, 1)]
+
+        def pick_last(u):
+            cols = slice(u * HALF, (u + 1) * HALF)
+            for t in range(PACK):
+                if t % 2 == 0:
+                    pair = half_row(*late[(u * PACK + t) // 2])
+                g1 = pair[:, (t % 2) * HALF : (t % 2 + 1) * HALF]
+                nc.vector.tensor_copy(g1, windows[last * PACK + t][:].indirect(pos1_t[:, u * HALF // 16 : (u + 1) * HALF // 16]))
+                if u * PACK + t >= X1S:
+                    nc.scalar.activation(x1_rows[last][:, t, cols], g1, ACT.Copy, scale=gain_t[:, last, t : t + 1])
+                else:
+                    nc.gpsimd.tensor_scalar(x1_rows[last][:, t, cols], g1, gain_t[:, last, t : t + 1], 0.0, ALU.mult, ALU.add)
+
+        def finish_last(m):
+            if m >= ILV:
+                dst, srcv = il_views(x1_il[last], x1_rows[last], m * P, (m + 1) * P)
+                nc.vector.tensor_copy(dst, srcv)
+            else:
+                interleave(x1_il[last], x1_rows[last], m * P, (m + 1) * P)
+            quantize(x1_codes[last], x1_sc[last], x1_il[last], m * P, (m + 1) * P)
+
+        def reference_out(m):
             second_pass(ref_ps, wr_codes, wr_sc, last, m)
-        for m in range(MT):
-            interleave(x1_il[last], x1_rows[last], m * P, (m + 1) * P)
             nc.scalar.copy(ref_sb[m][:], ref_ps[m][:])
-        for m in range(MT + 1):
-            if m < MT:
-                quantize(x1_codes[last], x1_sc[last], x1_il[last], m * P, (m + 1) * P)
-                second_pass(e_ps, x1_codes, x1_sc, last, m)
-            if m >= 1:
-                res = keep.tile([P, BANK], F32, name="res%d" % (m - 1))
-                nc.vector.tensor_tensor(res[:], e_ps[m - 1][:], ref_sb[m - 1][:], ALU.max)
-                nc.sync.dma_start(out[(m - 1) * P : m * P, :], res[:])
+
+        def score_out(m):
+            second_pass(e_ps, x1_codes, x1_sc, last, m)
+            res = keep.tile([P, BANK], F32, name="res%d" % m)
+            nc.vector.tensor_tensor(res[:], e_ps[m][:], ref_sb[m][:], ALU.max)
+            nc.sync.dma_start(out[m * P : (m + 1) * P, :], res[:])
+
+        pick_last(0)
+        pick_last(1)
+        for u in range(2):
+            for m in (2 * u, 2 * u + 1):
+                finish_last(m)
+            for m in (2 * u, 2 * u + 1):
+                reference_out(m)
+            for m in (2 * u, 2 * u + 1):
+                score_out(m)

@@ -25,17 +25,19 @@ HALVES = S // BANK
 MT = NP // P
 AHEAD = 3
 TXT = 3
-RING = 4
+RING = 5
 WINDOWS = 6
 X2S = 11
-WR_AT = [4, 7, 8]
+WR_AT = [3, 7, 9]
 LAG = 0
 X1S = 8
 ILV = 4
-CUT = 4
-CUTX = 2
+CUT = 1
+CUTX = 1
 W1_AT = 1
-TIE = 1
+WR_SLOT = "cab"
+F2 = 0
+F1 = 1
 
 
 def tile_list_pair_seat_harmony_kernel(
@@ -75,25 +77,23 @@ def tile_list_pair_seat_harmony_kernel(
         nc.sync.dma_start(offs_t[:], offs)
         nc.sync.dma_start(pos2_t[:], pos2)
         nc.sync.dma_start(pos1_t[:], pos1)
-        w2w_first = slot("a", [P, 2 * PASS], U8)
-        nc.sync.dma_start(w2w_first[:].bitcast(I32), w2_words[0][:, 0 : 2 * PASS].bitcast(I32))
+        w2w = slot("a", [P, 2 * H], U8)
+        nc.sync.dma_start(w2w[:].bitcast(I32), w2_words[0].bitcast(I32))
         nc.sync.dma_start(tabw[:].bitcast(I32), tab_words[0].rearrange("p t i -> p (t i)").bitcast(I32))
         w1_halves = [slot("b", [P, PACK, HALF], F32), slot("c", [P, PACK, HALF], F32)]
         for u in range(2):
             nc.sync.dma_start(w1_halves[u][:], w1_rows[:, :, u * HALF : (u + 1) * HALF])
         load_scales(nc.scalar, tabs, tab_scales[0])
 
-        def deal_w2(b, words):
-            nc.gpsimd.tensor_copy(
-                w2_codes[:, 2 * b * PASS : 2 * (b + 1) * PASS].rearrange("p (t q e) -> p t q e", t=PACK, e=2),
-                words.rearrange("p (q t e) -> p t q e", t=PACK, e=2),
-            )
+        nc.vector.tensor_copy(
+            w2_codes[:].rearrange("p (b t q e) -> p b t q e", b=NB, t=PACK, e=2),
+            w2w[:].rearrange("p (b q t e) -> p b t q e", b=NB, t=PACK, e=2),
+        )
+        for b in range(NB):
             nc.gpsimd.tensor_copy(
                 w2_sc[:, b * PASS : (b + 1) * PASS].rearrange("p (t q) -> p t q", t=PACK),
                 w2s[:, b * PASS : (b + 1) * PASS].rearrange("p (q t) -> p t q", t=PACK),
             )
-
-        deal_w2(0, w2w_first[:])
         nc.gpsimd.dma_start(gain_t[:], gain.rearrange("(b p t) -> p b t", p=P, t=PACK))
         nc.gpsimd.dma_start(dh_t[:], dh.rearrange("(b p t) -> p b t", p=P, t=PACK))
 
@@ -151,7 +151,7 @@ def tile_list_pair_seat_harmony_kernel(
             b, t = divmod(s, PACK)
             cols = slice(t * P, (t + 1) * P)
             c0 = b * PASS + t * P
-            win = keep.tile([P, S], F32, name="win%d" % (s % WINDOWS))
+            win = keep.tile([P, S], F32, name="win%d" % (s % WINDOWS), align_bytes=64)
             windows[s] = win
             for h in range(HALVES):
                 pa = psum.tile([P, BANK], F32, name="bank%d" % h)
@@ -172,7 +172,7 @@ def tile_list_pair_seat_harmony_kernel(
             b, t = divmod(s, PACK)
             if t == 0:
                 x1_rows[b] = new_rows("x1_rows")
-            g1 = keep.tile([P, NP], F32, name="size%d" % ((s - TIE) % (TIE + 2)))
+            g1 = half_row(s + 1, 1)
             nc.vector.tensor_copy(g1[:], windows[s][:].indirect(pos1_t[:]))
             nc.gpsimd.tensor_scalar(x1_rows[b][:, t, :], g1[:], gain_t[:, b, t : t + 1], 0.0, ALU.mult, ALU.add)
 
@@ -182,7 +182,7 @@ def tile_list_pair_seat_harmony_kernel(
                 x2_rows[b] = new_rows("x2_rows")
             g2 = half_row(s + 1, 0)
             nc.vector.tensor_copy(g2[:], windows[s][:].indirect(pos2_t[:]))
-            size = keep.tile([P, NP], F32, name="size%d" % (s % (TIE + 2)))
+            size = ring.tile([P, NP], F32, name="size")
             nc.scalar.activation(size[:], g2[:], ACT.Abs, scale=gain_t[:, b, t : t + 1])
             if s >= X2S:
                 nc.scalar.activation(x2_rows[b][:, t, :], size[:], ACT.Copy, scale=dh_t[:, b, t : t + 1])
@@ -190,7 +190,7 @@ def tile_list_pair_seat_harmony_kernel(
                 nc.gpsimd.tensor_scalar(x2_rows[b][:, t, :], size[:], dh_t[:, b, t : t + 1], 0.0, ALU.mult, ALU.add)
 
         def prepare_w1(b):
-            raw = slot("a" if b == 1 else "c", [P, PACK, PASS], F32)
+            raw = slot("ab"[b - 1 : b], [P, PACK, PASS], F32)
             nc.sync.dma_start(raw[:], w1_rows[:, :, b * PASS : (b + 1) * PASS])
             w1_il[b] = new_il("w1_il")
             for u in range(CUT):
@@ -199,18 +199,21 @@ def tile_list_pair_seat_harmony_kernel(
             quantize(w1_codes[b], w1_sc[b], w1_il[b], 0, PASS)
 
         def prepare_wr(b):
-            raw = slot("aca"[b : b + 1], [P, PACK, NP], F32)
+            raw = slot(WR_SLOT[b : b + 1], [P, PACK, NP], F32)
             nc.sync.dma_start(raw[:], wr_rows[b])
             wr_il[b] = new_il("wr_il")
             for u in range(CUT):
                 interleave(wr_il[b], raw, u * NP // CUT, (u + 1) * NP // CUT)
             quantize(wr_codes[b], wr_sc[b], wr_il[b], 0, NP)
 
-        def finish(il, name, rows, codes, sc, b):
-            il[b] = new_il(name)
+        def finish(il, s, rows, codes, sc, b):
+            il[b] = keep.tile([P, PACK * NP], BF16, name="win%d" % (s % WINDOWS), align_bytes=64)
             for u in range(CUTX):
                 interleave(il[b], rows[b], u * NP // CUTX, (u + 1) * NP // CUTX)
             quantize(codes[b], sc[b], il[b], 0, NP)
+
+        def tied(s):
+            return s if s < last * PACK else s - PACK + 2
 
         w1_il[0] = slot("d", [P, PACK * PASS], BF16)
         for u in range(2):
@@ -218,10 +221,6 @@ def tile_list_pair_seat_harmony_kernel(
         quantize(w1_codes[0], w1_sc[0], w1_il[0], 0, PASS)
         v_sc.append(slot("d", [P, BANK], U8))
         nc.vector.tensor_copy(v_sc[1][:], tabs[:].indirect(parts[1]))
-        w2w_rest = slot("b", [P, 2 * (H - PASS)], U8)
-        nc.sync.dma_start(w2w_rest[:].bitcast(I32), w2_words[0][:, 2 * PASS : 2 * H].bitcast(I32))
-        for b in range(1, NB):
-            deal_w2(b, w2w_rest[:, 2 * (b - 1) * PASS : 2 * b * PASS])
 
         for i in range(slices + TXT):
             if i < slices:
@@ -236,10 +235,10 @@ def tile_list_pair_seat_harmony_kernel(
                 pick_x2(s)
                 if LAG <= s and s - LAG < last * PACK:
                     pick_x1(s - LAG)
-                if t == PACK - 1:
-                    finish(x2_il, "x2_il", x2_rows, x2_codes, x2_sc, b)
-                    if b < last:
-                        finish(x1_il, "x1_il", x1_rows, x1_codes, x1_sc, b)
+                if b >= 1 and t == F2:
+                    finish(x2_il, tied(s), x2_rows, x2_codes, x2_sc, b - 1)
+                if b >= 1 and t == F1:
+                    finish(x1_il, tied(s), x1_rows, x1_codes, x1_sc, b - 1)
 
         ref_ps = [psum.tile([P, BANK], F32, name="bank%d" % m) for m in range(MT)]
         e_ps = [psum.tile([P, BANK], F32, name="bank%d" % (MT + m)) for m in range(MT)]
@@ -251,8 +250,8 @@ def tile_list_pair_seat_harmony_kernel(
                 rhs=x2_codes[b][:].bitcast(FP8X4), rhs_scale=x2_sc[b][:], start=(b == 0), stop=(b == last),
             )
 
-        for acc, codes, sc in ((ref_ps, wr_codes, wr_sc), (e_ps, x1_codes, x1_sc)):
-            for b in range(last):
+        for b in range(last):
+            for acc, codes, sc in ((ref_ps, wr_codes, wr_sc), (e_ps, x1_codes, x1_sc)):
                 for m in range(MT):
                     second_pass(acc, codes, sc, b, m)
 
@@ -292,6 +291,7 @@ def tile_list_pair_seat_harmony_kernel(
             nc.vector.tensor_tensor(res[:], e_ps[m][:], ref_sb[m][:], ALU.max)
             nc.sync.dma_start(out[m * P : (m + 1) * P, :], res[:])
 
+        finish(x2_il, slices, x2_rows, x2_codes, x2_sc, last)
         pick_last(0)
         pick_last(1)
         for u in range(2):

@@ -27,11 +27,11 @@ AHEAD = 3
 TXT = 3
 RING = 5
 WINDOWS = 6
-X2S = 11
+X2S = 4
 WR_AT = [3, 7, 9]
 LAG = 0
-X1S = 8
-ILV = 4
+X1S = 0
+ILV = 2
 CUT = 1
 CUTX = 1
 W1_AT = 1
@@ -58,7 +58,7 @@ def tile_list_pair_seat_harmony_kernel(
         gain_t = keep.tile([P, NB, PACK], F32, name="gain_t")
         dh_t = keep.tile([P, NB, PACK], F32, name="dh_t")
         w2_codes = keep.tile([P, 2 * H], U8, name="w2_codes", align_bytes=64)
-        w2_sc = keep.tile([P, H], U8, name="w2_sc", align_bytes=64)
+        w2_sc = [keep.tile([P, PASS], U8, name="w2_sc", align_bytes=64)]
 
         def slot(name, shape, dtype):
             return keep.tile(shape, dtype, name="slot_" + name, align_bytes=64)
@@ -89,11 +89,10 @@ def tile_list_pair_seat_harmony_kernel(
             w2_codes[:].rearrange("p (b t q e) -> p b t q e", b=NB, t=PACK, e=2),
             w2w[:].rearrange("p (b q t e) -> p b t q e", b=NB, t=PACK, e=2),
         )
-        for b in range(NB):
-            nc.gpsimd.tensor_copy(
-                w2_sc[:, b * PASS : (b + 1) * PASS].rearrange("p (t q) -> p t q", t=PACK),
-                w2s[:, b * PASS : (b + 1) * PASS].rearrange("p (q t) -> p t q", t=PACK),
-            )
+        nc.vector.tensor_copy(
+            w2_sc[0][:].rearrange("p (t q) -> p t q", t=PACK),
+            w2s[:, 0:PASS].rearrange("p (q t) -> p t q", t=PACK),
+        )
         nc.gpsimd.dma_start(gain_t[:], gain.rearrange("(b p t) -> p b t", p=P, t=PACK))
         nc.gpsimd.dma_start(dh_t[:], dh.rearrange("(b p t) -> p b t", p=P, t=PACK))
 
@@ -161,7 +160,7 @@ def tile_list_pair_seat_harmony_kernel(
                     rhs=v_codes[h][:].bitcast(FP8X4), rhs_scale=v_sc[h][:], start=True, stop=True,
                 )
                 nc.tensor.matmul_mx(
-                    out=pl[:], lhsT=w2_codes[:, 2 * c0 : 2 * (c0 + P)].bitcast(FP4X4), lhsT_scale=w2_sc[:, c0 : c0 + P],
+                    out=pl[:], lhsT=w2_codes[:, 2 * c0 : 2 * (c0 + P)].bitcast(FP4X4), lhsT_scale=w2_sc[b][:, cols],
                     rhs=v_codes[h][:].bitcast(FP8X4), rhs_scale=v_sc[h][:], start=True, stop=True,
                 )
                 bounded = half_row(s, h)
@@ -174,7 +173,7 @@ def tile_list_pair_seat_harmony_kernel(
                 x1_rows[b] = new_rows("x1_rows")
             g1 = half_row(s + 1, 1)
             nc.vector.tensor_copy(g1[:], windows[s][:].indirect(pos1_t[:]))
-            nc.gpsimd.tensor_scalar(x1_rows[b][:, t, :], g1[:], gain_t[:, b, t : t + 1], 0.0, ALU.mult, ALU.add)
+            nc.scalar.activation(x1_rows[b][:, t, :], g1[:], ACT.Copy, scale=gain_t[:, b, t : t + 1])
 
         def pick_x2(s):
             b, t = divmod(s, PACK)
@@ -184,10 +183,10 @@ def tile_list_pair_seat_harmony_kernel(
             nc.vector.tensor_copy(g2[:], windows[s][:].indirect(pos2_t[:]))
             size = ring.tile([P, NP], F32, name="size")
             nc.scalar.activation(size[:], g2[:], ACT.Abs, scale=gain_t[:, b, t : t + 1])
-            if s >= X2S:
+            if s < X2S:
                 nc.scalar.activation(x2_rows[b][:, t, :], size[:], ACT.Copy, scale=dh_t[:, b, t : t + 1])
             else:
-                nc.gpsimd.tensor_scalar(x2_rows[b][:, t, :], size[:], dh_t[:, b, t : t + 1], 0.0, ALU.mult, ALU.add)
+                nc.vector.tensor_scalar(x2_rows[b][:, t, :], size[:], dh_t[:, b, t : t + 1], None, ALU.mult)
 
         def prepare_w1(b):
             raw = slot("ab"[b - 1 : b], [P, PACK, PASS], F32)
@@ -221,6 +220,12 @@ def tile_list_pair_seat_harmony_kernel(
         quantize(w1_codes[0], w1_sc[0], w1_il[0], 0, PASS)
         v_sc.append(slot("d", [P, BANK], U8))
         nc.vector.tensor_copy(v_sc[1][:], tabs[:].indirect(parts[1]))
+        w2_sc_rest = keep.tile([P, H - PASS], U8, name="tabs", align_bytes=64)
+        nc.vector.tensor_copy(
+            w2_sc_rest[:].rearrange("p (b t q) -> p b t q", t=PACK, q=P),
+            w2s[:, PASS:H].rearrange("p (b q t) -> p b t q", t=PACK, q=P),
+        )
+        w2_sc.extend([w2_sc_rest[:, 0:PASS], w2_sc_rest[:, PASS : 2 * PASS]])
 
         for i in range(slices + TXT):
             if i < slices:
@@ -271,7 +276,7 @@ def tile_list_pair_seat_harmony_kernel(
                 if u * PACK + t >= X1S:
                     nc.scalar.activation(x1_rows[last][:, t, cols], g1, ACT.Copy, scale=gain_t[:, last, t : t + 1])
                 else:
-                    nc.gpsimd.tensor_scalar(x1_rows[last][:, t, cols], g1, gain_t[:, last, t : t + 1], 0.0, ALU.mult, ALU.add)
+                    nc.vector.tensor_scalar(x1_rows[last][:, t, cols], g1, gain_t[:, last, t : t + 1], None, ALU.mult)
 
         def finish_last(m):
             if m >= ILV:

from contextlib import ExitStack

import concourse.mybir as mybir

K, H, T, S, NP = 512, 1536, 4096, 1024, 512
FLOPS = 2 * 2 * K * H * S + 2 * 2 * H * NP * NP

F32 = mybir.dt.float32
BF16 = mybir.dt.bfloat16
I32 = mybir.dt.int32
U32 = mybir.dt.uint32
U16 = mybir.dt.uint16
U8 = mybir.dt.uint8
FP8X4 = mybir.dt.float8_e4m3fn_x4
FP4X4 = mybir.dt.float4_e2m1fn_x4
ACT = mybir.ActivationFunctionType
ALU = mybir.AluOpType

P = 128
PACK = 4
PASS = P * PACK
NB = H // PASS
BANK = 512
HALVES = S // BANK
MT = NP // P
AHEAD = 3
TXT = 3
RING = 5
WINDOWS = 6
X2S = 4
WR_AT = [3, 7, 9]
LAG = 0
X1S = 0
ILV = 2
CUT = 1
CUTX = 1
W1_AT = 1
WR_SLOT = "cab"
F2 = 0
F1 = 1


def tile_list_pair_seat_harmony_kernel(
    tc, tab_words, tab_scales, offs, pos1, pos2, w1, w2_words, w2_scales, gain, dh, wr, out
):
    nc = tc.nc
    with ExitStack() as ctx:
        keep = ctx.enter_context(tc.tile_pool(name="keep", bufs=1))
        ring = ctx.enter_context(tc.tile_pool(name="ring", bufs=2))
        psum = ctx.enter_context(tc.psum_pool(name="psum", bufs=1))

        offs_t = keep.tile([P, S // 16], U16, name="offs_t")
        pos1_t = keep.tile([P, NP // 16], U16, name="pos1_t")
        pos2_t = keep.tile([P, NP // 16], U16, name="pos2_t")
        tabw = keep.tile([P, T], U32, name="tabw", align_bytes=64)
        tabs = keep.tile([P, T], U8, name="tabs", align_bytes=64)
        w2s = keep.tile([P, H], U8, name="w2s", align_bytes=64)
        gain_t = keep.tile([P, NB, PACK], F32, name="gain_t")
        dh_t = keep.tile([P, NB, PACK], F32, name="dh_t")
        w2_codes = keep.tile([P, 2 * H], U8, name="w2_codes", align_bytes=64)
        w2_sc = [keep.tile([P, PASS], U8, name="w2_sc", align_bytes=64)]

        def slot(name, shape, dtype):
            return keep.tile(shape, dtype, name="slot_" + name, align_bytes=64)

        def load_scales(queue, tile, rows):
            for q in range(4):
                queue.dma_start(tile[32 * q : 32 * q + 4, :].bitcast(I32), rows[4 * q : 4 * q + 4, :].bitcast(I32))

        w1_rows = w1.rearrange("(p j) c -> p j c", j=PACK)
        wr_rows = wr.rearrange("(b p j) m -> b p j m", p=P, j=PACK)
        HALF = PASS // 2

        nc.gpsimd.memset(w2s[:].bitcast(I32), 0)
        nc.vector.memset(tabs[:].bitcast(I32), 0)
        load_scales(nc.gpsimd, w2s, w2_scales[0])
        nc.sync.dma_start(offs_t[:], offs)
        nc.sync.dma_start(pos2_t[:], pos2)
        nc.sync.dma_start(pos1_t[:], pos1)
        w2w = slot("a", [P, 2 * H], U8)
        nc.sync.dma_start(w2w[:].bitcast(I32), w2_words[0].bitcast(I32))
        nc.sync.dma_start(tabw[:].bitcast(I32), tab_words[0].rearrange("p t i -> p (t i)").bitcast(I32))
        w1_halves = [slot("b", [P, PACK, HALF], F32), slot("c", [P, PACK, HALF], F32)]
        for u in range(2):
            nc.sync.dma_start(w1_halves[u][:], w1_rows[:, :, u * HALF : (u + 1) * HALF])
        load_scales(nc.scalar, tabs, tab_scales[0])

        nc.vector.tensor_copy(
            w2_codes[:].rearrange("p (b t q e) -> p b t q e", b=NB, t=PACK, e=2),
            w2w[:].rearrange("p (b q t e) -> p b t q e", b=NB, t=PACK, e=2),
        )
        nc.vector.tensor_copy(
            w2_sc[0][:].rearrange("p (t q) -> p t q", t=PACK),
            w2s[:, 0:PASS].rearrange("p (q t) -> p t q", t=PACK),
        )
        nc.gpsimd.dma_start(gain_t[:], gain.rearrange("(b p t) -> p b t", p=P, t=PACK))
        nc.gpsimd.dma_start(dh_t[:], dh.rearrange("(b p t) -> p b t", p=P, t=PACK))

        v_codes = [keep.tile([P, BANK], U32, name="v_codes%d" % h, align_bytes=64) for h in range(HALVES)]
        per = BANK // 16
        parts = [offs_t[:, h * per : (h + 1) * per] for h in range(HALVES)]
        for h in range(HALVES):
            nc.vector.tensor_copy(v_codes[h][:], tabw[:].indirect(parts[h]))
        v_sc = [keep.tile([P, BANK], U8, name="v_sc0", align_bytes=64)]
        nc.vector.tensor_copy(v_sc[0][:], tabs[:].indirect(parts[0]))

        def planes(name, width):
            codes = [keep.tile([P, width], U32, name="%s_codes%d" % (name, b), align_bytes=64) for b in range(NB)]
            sc = [keep.tile([P, width], U8, name="%s_sc%d" % (name, b), align_bytes=64) for b in range(NB)]
            return codes, sc

        w1_codes, w1_sc = planes("w1", PASS)
        wr_codes, wr_sc = planes("wr", NP)
        x1_codes, x1_sc = planes("x1", NP)
        x2_codes, x2_sc = planes("x2", NP)
        w1_il, wr_il, x1_il, x2_il, x1_rows, x2_rows = {}, {}, {}, {}, {}, {}

        def new_il(name):
            return ring.tile([P, PACK * NP], BF16, name=name, align_bytes=64)

        def new_rows(name):
            return ring.tile([P, PACK, NP], BF16, name=name)

        def quantize(codes, sc, il, c0, c1):
            nc.vector.quantize_mx(out=codes[:, c0:c1].bitcast(FP8X4), scales=sc[:, c0:c1], in_=il[:, PACK * c0 : PACK * c1])

        def cast_w1(b, raw, q0, q1):
            nc.scalar.copy(
                w1_il[b][:].rearrange("p (t q j) -> p q j t", t=PACK, j=PACK)[:, q0:q1],
                raw.rearrange("p j (q t) -> p q j t", t=PACK),
            )

        def il_views(il, rows, c0, c1):
            dst = il[:, PACK * c0 : PACK * c1].rearrange("p (c i t) -> p c t i", i=4, t=PACK)
            srcv = rows[:, :, c0:c1].rearrange("p t (c i) -> p c t i", i=4)
            return dst, srcv

        def interleave(il, rows, c0, c1):
            dst, srcv = il_views(il, rows, c0, c1)
            nc.scalar.copy(dst, srcv)

        windows = {}
        slices = NB * PACK
        last = NB - 1

        def half_row(s, h):
            return keep.tile([P, BANK], F32, name="half%d_%d" % (s % RING, h))

        def first_stage(s):
            b, t = divmod(s, PACK)
            cols = slice(t * P, (t + 1) * P)
            c0 = b * PASS + t * P
            win = keep.tile([P, S], F32, name="win%d" % (s % WINDOWS), align_bytes=64)
            windows[s] = win
            for h in range(HALVES):
                pa = psum.tile([P, BANK], F32, name="bank%d" % h)
                pl = psum.tile([P, BANK], F32, name="bank%d" % (HALVES * (1 + s % AHEAD) + h))
                nc.tensor.matmul_mx(
                    out=pa[:], lhsT=w1_codes[b][:, cols].bitcast(FP8X4), lhsT_scale=w1_sc[b][:, cols],
                    rhs=v_codes[h][:].bitcast(FP8X4), rhs_scale=v_sc[h][:], start=True, stop=True,
                )
                nc.tensor.matmul_mx(
                    out=pl[:], lhsT=w2_codes[:, 2 * c0 : 2 * (c0 + P)].bitcast(FP4X4), lhsT_scale=w2_sc[b][:, cols],
                    rhs=v_codes[h][:].bitcast(FP8X4), rhs_scale=v_sc[h][:], start=True, stop=True,
                )
                bounded = half_row(s, h)
                nc.scalar.activation(bounded[:], pa[:], ACT.Tanh)
                nc.vector.tensor_tensor(win[:, h * BANK : (h + 1) * BANK], pl[:], bounded[:], ALU.add)

        def pick_x1(s):
            b, t = divmod(s, PACK)
            if t == 0:
                x1_rows[b] = new_rows("x1_rows")
            g1 = half_row(s + 1, 1)
            nc.vector.tensor_copy(g1[:], windows[s][:].indirect(pos1_t[:]))
            nc.scalar.activation(x1_rows[b][:, t, :], g1[:], ACT.Copy, scale=gain_t[:, b, t : t + 1])

        def pick_x2(s):
            b, t = divmod(s, PACK)
            if t == 0:
                x2_rows[b] = new_rows("x2_rows")
            g2 = half_row(s + 1, 0)
            nc.vector.tensor_copy(g2[:], windows[s][:].indirect(pos2_t[:]))
            size = ring.tile([P, NP], F32, name="size")
            nc.scalar.activation(size[:], g2[:], ACT.Abs, scale=gain_t[:, b, t : t + 1])
            if s < X2S:
                nc.scalar.activation(x2_rows[b][:, t, :], size[:], ACT.Copy, scale=dh_t[:, b, t : t + 1])
            else:
                nc.vector.tensor_scalar(x2_rows[b][:, t, :], size[:], dh_t[:, b, t : t + 1], None, ALU.mult)

        def prepare_w1(b):
            raw = slot("ab"[b - 1 : b], [P, PACK, PASS], F32)
            nc.sync.dma_start(raw[:], w1_rows[:, :, b * PASS : (b + 1) * PASS])
            w1_il[b] = new_il("w1_il")
            for u in range(CUT):
                q0, q1 = u * P // CUT, (u + 1) * P // CUT
                cast_w1(b, raw[:, :, PACK * q0 : PACK * q1], q0, q1)
            quantize(w1_codes[b], w1_sc[b], w1_il[b], 0, PASS)

        def prepare_wr(b):
            raw = slot(WR_SLOT[b : b + 1], [P, PACK, NP], F32)
            nc.sync.dma_start(raw[:], wr_rows[b])
            wr_il[b] = new_il("wr_il")
            for u in range(CUT):
                interleave(wr_il[b], raw, u * NP // CUT, (u + 1) * NP // CUT)
            quantize(wr_codes[b], wr_sc[b], wr_il[b], 0, NP)

        def finish(il, s, rows, codes, sc, b):
            il[b] = keep.tile([P, PACK * NP], BF16, name="win%d" % (s % WINDOWS), align_bytes=64)
            for u in range(CUTX):
                interleave(il[b], rows[b], u * NP // CUTX, (u + 1) * NP // CUTX)
            quantize(codes[b], sc[b], il[b], 0, NP)

        def tied(s):
            return s if s < last * PACK else s - PACK + 2

        w1_il[0] = slot("d", [P, PACK * PASS], BF16)
        for u in range(2):
            cast_w1(0, w1_halves[u][:], u * P // 2, (u + 1) * P // 2)
        quantize(w1_codes[0], w1_sc[0], w1_il[0], 0, PASS)
        v_sc.append(slot("d", [P, BANK], U8))
        nc.vector.tensor_copy(v_sc[1][:], tabs[:].indirect(parts[1]))
        w2_sc_rest = keep.tile([P, H - PASS], U8, name="tabs", align_bytes=64)
        nc.vector.tensor_copy(
            w2_sc_rest[:].rearrange("p (b t q) -> p b t q", t=PACK, q=P),
            w2s[:, PASS:H].rearrange("p (b q t) -> p b t q", t=PACK, q=P),
        )
        w2_sc.extend([w2_sc_rest[:, 0:PASS], w2_sc_rest[:, PASS : 2 * PASS]])

        for i in range(slices + TXT):
            if i < slices:
                first_stage(i)
                if i % PACK == W1_AT and i // PACK < last:
                    prepare_w1(i // PACK + 1)
                if i in WR_AT:
                    prepare_wr(WR_AT.index(i))
            s = i - TXT
            if s >= 0:
                b, t = divmod(s, PACK)
                pick_x2(s)
                if LAG <= s and s - LAG < last * PACK:
                    pick_x1(s - LAG)
                if b >= 1 and t == F2:
                    finish(x2_il, tied(s), x2_rows, x2_codes, x2_sc, b - 1)
                if b >= 1 and t == F1:
                    finish(x1_il, tied(s), x1_rows, x1_codes, x1_sc, b - 1)

        ref_ps = [psum.tile([P, BANK], F32, name="bank%d" % m) for m in range(MT)]
        e_ps = [psum.tile([P, BANK], F32, name="bank%d" % (MT + m)) for m in range(MT)]

        def second_pass(acc, codes, sc, b, m):
            cols = slice(m * P, (m + 1) * P)
            nc.tensor.matmul_mx(
                out=acc[m][:], lhsT=codes[b][:, cols].bitcast(FP8X4), lhsT_scale=sc[b][:, cols],
                rhs=x2_codes[b][:].bitcast(FP8X4), rhs_scale=x2_sc[b][:], start=(b == 0), stop=(b == last),
            )

        for b in range(last):
            for acc, codes, sc in ((ref_ps, wr_codes, wr_sc), (e_ps, x1_codes, x1_sc)):
                for m in range(MT):
                    second_pass(acc, codes, sc, b, m)

        x1_rows[last] = new_rows("x1_rows")
        x1_il[last] = new_il("x1_il")
        ref_sb = [keep.tile([P, BANK], F32, name="ref%d" % m) for m in range(MT)]

        late = [(slices - 1, 1), (slices - 1, 0), (slices, 0), (slices - 1, 1)]

        def pick_last(u):
            cols = slice(u * HALF, (u + 1) * HALF)
            for t in range(PACK):
                if t % 2 == 0:
                    pair = half_row(*late[(u * PACK + t) // 2])
                g1 = pair[:, (t % 2) * HALF : (t % 2 + 1) * HALF]
                nc.vector.tensor_copy(g1, windows[last * PACK + t][:].indirect(pos1_t[:, u * HALF // 16 : (u + 1) * HALF // 16]))
                if u * PACK + t >= X1S:
                    nc.scalar.activation(x1_rows[last][:, t, cols], g1, ACT.Copy, scale=gain_t[:, last, t : t + 1])
                else:
                    nc.vector.tensor_scalar(x1_rows[last][:, t, cols], g1, gain_t[:, last, t : t + 1], None, ALU.mult)

        def finish_last(m):
            if m >= ILV:
                dst, srcv = il_views(x1_il[last], x1_rows[last], m * P, (m + 1) * P)
                nc.vector.tensor_copy(dst, srcv)
            else:
                interleave(x1_il[last], x1_rows[last], m * P, (m + 1) * P)
            quantize(x1_codes[last], x1_sc[last], x1_il[last], m * P, (m + 1) * P)

        def reference_out(m):
            second_pass(ref_ps, wr_codes, wr_sc, last, m)
            nc.scalar.copy(ref_sb[m][:], ref_ps[m][:])

        def score_out(m):
            second_pass(e_ps, x1_codes, x1_sc, last, m)
            res = keep.tile([P, BANK], F32, name="res%d" % m)
            nc.vector.tensor_tensor(res[:], e_ps[m][:], ref_sb[m][:], ALU.max)
            nc.sync.dma_start(out[m * P : (m + 1) * P, :], res[:])

        finish(x2_il, slices, x2_rows, x2_codes, x2_sc, last)
        pick_last(0)
        pick_last(1)
        for u in range(2):
            for m in (2 * u, 2 * u + 1):
                finish_last(m)
            for m in (2 * u, 2 * u + 1):
                reference_out(m)
            for m in (2 * u, 2 * u + 1):
                score_out(m)
